import numpy as np
CORES = [1,9,17,25,33,41,49,57,65,73,81,89,97,105,113,121]
N = 16
ROWS, COLS = 4, 4
def setup_inputs(rng):
    return {"x": rng.standard_normal((N, 128, 128), dtype=np.float32)}
def reference(x):
    g = x.astype(np.float64).reshape(ROWS, COLS, 128, 128)
    rs = g.sum(axis=1)
    cs = g.sum(axis=0)
    y1 = np.stack([rs[r // COLS] for r in range(N)]).astype(x.dtype)
    y2 = np.stack([cs[r % COLS] for r in range(N)]).astype(x.dtype)
    return {"y1": y1, "y2": y2}

@@ -1,0 +1,70 @@
+from concourse.bass import DstId, RemoteDMATransfer
+from concourse.mybir import AluOpType
+
+MEM = "sbuf"
+BUF = (MEM, [128, 128], "float32")
+SCRATCH = {
+    "xs": BUF,
+    "rp": BUF,
+    "pm": BUF,
+    "c1": BUF, "c2": BUF, "c3": BUF,
+    "ha": BUF, "hb": BUF,
+}
+SEMAPHORES = ["ld", "k1", "k2", "k3", "rin", "cin", "pin", "sent"]
+
+RANK_CORE, PORT_CORE = 1, 2
+
+
+def rank_program(g, core, T, topo):
+    chip, k = core // 8, core % 8
+    s = T.sem
+    add = AluOpType.add
+
+    def dst(c):
+        rid, pid, se = topo.addr(c)
+        return DstId(rid=rid, pnc=pid)
+
+    if k == PORT_CORE:
+        g.wait_ge(s.rin, 12)
+        g.remote_dma_fused([
+            RemoteDMATransfer(dst_ids=[dst((chip ^ 1) * 8 + RANK_CORE)], dma_engine_mask=0x00FF, remote_sem=s.pin,
+                              srcs=[T.ha[:], T.hb[:]], dsts=[T.pm[:]], alu_op=1),
+        ], local_sem=s.sent)
+        g.wait_ge(s.sent, 8)
+        return
+    if k != RANK_CORE:
+        return
+
+    r = T.rank_of(core)
+    peer = T.cores[r ^ 2]
+    cols = [T.cores[(r + 4 * j) % 16] for j in (1, 2, 3)]
+
+    g.dma_start(out=T.xs[:], in_=T.x[:]).then_inc(s.ld, 16)
+    g.dma_start(out=T.y1[:], in_=T.x[:]).then_inc(s.k1, 16)
+    g.dma_start(out=T.y2[:], in_=T.x[:]).then_inc(s.k2, 16)
+    g.wait_ge(s.ld, 16)
+    g.remote_dma_fused([
+        RemoteDMATransfer(dst_ids=[dst(chip * 8 + PORT_CORE)], dma_engine_mask=0xFF00, remote_sem=s.rin,
+                          srcs=[T.xs[:]], dsts=[T.ha[:]]),
+        RemoteDMATransfer(dst_ids=[dst(peer - RANK_CORE + PORT_CORE), dst(peer)], dma_engine_mask=0x000F,
+                          remote_sem=s.rin, srcs=[T.xs[:]], dsts=[T.hb[:], T.rp[:]]),
+        RemoteDMATransfer(dst_ids=[dst(c) for c in cols], dma_engine_mask=0x00F0, remote_sem=s.cin,
+                          srcs=[T.xs[:]], dsts=[T.c1[:], T.c2[:], T.c3[:]]),
+    ], local_sem=s.sent)
+
+    g.wait_ge(s.rin, 4)
+    g.wait_ge(s.k1, 16)
+    g.dma_start(out=T.y1[:], in_=T.rp[:], accum_op=add).then_inc(s.k1, 16)
+    g.wait_ge(s.cin, 12)
+    g.wait_ge(s.k2, 16)
+    g.dma_start(out=T.y2[:], in_=T.c1[:], accum_op=add).then_inc(s.k2, 16)
+    g.dma_start(out=T.c2[:], in_=T.c3[:], accum_op=add).then_inc(s.k3, 16)
+    g.wait_ge(s.k2, 32)
+    g.wait_ge(s.k3, 16)
+    g.dma_start(out=T.y2[:], in_=T.c2[:], accum_op=add).then_inc(s.k2, 16)
+    g.wait_ge(s.pin, 8)
+    g.wait_ge(s.k1, 32)
+    g.dma_start(out=T.y1[:], in_=T.pm[:], accum_op=add).then_inc(s.k1, 16)
+    g.wait_ge(s.k1, 48)
+    g.wait_ge(s.k2, 48)
+    g.wait_ge(s.sent, 16)

@@ -1,7 +1,7 @@
 from concourse.bass import DstId, RemoteDMATransfer
 from concourse.mybir import AluOpType
 
-MEM = "sbuf"
+MEM = "dram"
 BUF = (MEM, [128, 128], "float32")
 SCRATCH = {
     "xs": BUF,
@@ -54,17 +54,17 @@ def rank_program(g, core, T, topo):
 
     g.wait_ge(s.rin, 4)
     g.wait_ge(s.k1, 16)
-    g.dma_start(out=T.y1[:], in_=T.rp[:], accum_op=add).then_inc(s.k1, 16)
+    g.dma_start(out=T.y1[:], in_=T.rp[:], accum_op=add, max_dma_last_dim=8192).then_inc(s.k1, 16)
     g.wait_ge(s.cin, 12)
     g.wait_ge(s.k2, 16)
-    g.dma_start(out=T.y2[:], in_=T.c1[:], accum_op=add).then_inc(s.k2, 16)
-    g.dma_start(out=T.c2[:], in_=T.c3[:], accum_op=add).then_inc(s.k3, 16)
+    g.dma_start(out=T.y2[:], in_=T.c1[:], accum_op=add, max_dma_last_dim=8192).then_inc(s.k2, 16)
+    g.dma_start(out=T.c2[:], in_=T.c3[:], accum_op=add, max_dma_last_dim=8192).then_inc(s.k3, 16)
     g.wait_ge(s.k2, 32)
     g.wait_ge(s.k3, 16)
-    g.dma_start(out=T.y2[:], in_=T.c2[:], accum_op=add).then_inc(s.k2, 16)
+    g.dma_start(out=T.y2[:], in_=T.c2[:], accum_op=add, max_dma_last_dim=8192).then_inc(s.k2, 16)
     g.wait_ge(s.pin, 8)
     g.wait_ge(s.k1, 32)
-    g.dma_start(out=T.y1[:], in_=T.pm[:], accum_op=add).then_inc(s.k1, 16)
+    g.dma_start(out=T.y1[:], in_=T.pm[:], accum_op=add, max_dma_last_dim=8192).then_inc(s.k1, 16)
     g.wait_ge(s.k1, 48)
     g.wait_ge(s.k2, 48)
     g.wait_ge(s.sent, 16)

@@ -1,70 +1,79 @@
 from concourse.bass import DstId, RemoteDMATransfer
 from concourse.mybir import AluOpType
 
-MEM = "dram"
-BUF = (MEM, [128, 128], "float32")
+BUF = ("dram", [4, 128, 32], "float32")
 SCRATCH = {
     "xs": BUF,
     "rp": BUF,
     "pm": BUF,
-    "c1": BUF, "c2": BUF, "c3": BUF,
+    "ys": BUF,
     "ha": BUF, "hb": BUF,
+    "cq": BUF,
 }
-SEMAPHORES = ["ld", "k1", "k2", "k3", "rin", "cin", "pin", "sent"]
+SEMAPHORES = ["ld", "k1", "k2", "rin", "cin", "pin", "sent"]
 
-RANK_CORE, PORT_CORE = 1, 2
+RANK_CORE, PORT_CORE, COL_CORE = 1, 2, 4
 
 
 def rank_program(g, core, T, topo):
     chip, k = core // 8, core % 8
     s = T.sem
     add = AluOpType.add
+    row, col = chip // 4, chip % 4
 
-    def dst(c):
-        rid, pid, se = topo.addr(c)
+    def dst(ch, kk):
+        rid, pid, se = topo.addr(ch * 8 + kk)
         return DstId(rid=rid, pnc=pid)
 
     if k == PORT_CORE:
-        g.wait_ge(s.rin, 12)
+        g.wait_ge(s.rin, 16)
         g.remote_dma_fused([
-            RemoteDMATransfer(dst_ids=[dst((chip ^ 1) * 8 + RANK_CORE)], dma_engine_mask=0x00FF, remote_sem=s.pin,
-                              srcs=[T.ha[:], T.hb[:]], dsts=[T.pm[:]], alu_op=1),
+            RemoteDMATransfer(dst_ids=[dst(chip ^ 1, RANK_CORE)], dma_engine_mask=3 << (2 * q), remote_sem=s.pin,
+                              srcs=[T.ha[q], T.hb[q]], dsts=[T.pm[q]], alu_op=1)
+            for q in range(4)], local_sem=s.sent)
+        g.wait_ge(s.sent, 8)
+        return
+    if k == COL_CORE:
+        g.wait_ge(s.rin, 8)
+        others = [i for i in range(4) if i != row]
+        g.remote_dma_fused([
+            RemoteDMATransfer(dst_ids=[dst(4 * i + col, RANK_CORE) for i in others + [row]], dma_engine_mask=0x00FF,
+                              remote_sem=s.cin, srcs=[T.cq[i] for i in range(4)], dsts=[T.ys[row]] * 4, alu_op=1),
         ], local_sem=s.sent)
         g.wait_ge(s.sent, 8)
         return
     if k != RANK_CORE:
         return
 
-    r = T.rank_of(core)
-    peer = T.cores[r ^ 2]
-    cols = [T.cores[(r + 4 * j) % 16] for j in (1, 2, 3)]
-
     g.dma_start(out=T.xs[:], in_=T.x[:]).then_inc(s.ld, 16)
     g.dma_start(out=T.y1[:], in_=T.x[:]).then_inc(s.k1, 16)
-    g.dma_start(out=T.y2[:], in_=T.x[:]).then_inc(s.k2, 16)
     g.wait_ge(s.ld, 16)
-    g.remote_dma_fused([
-        RemoteDMATransfer(dst_ids=[dst(chip * 8 + PORT_CORE)], dma_engine_mask=0xFF00, remote_sem=s.rin,
-                          srcs=[T.xs[:]], dsts=[T.ha[:]]),
-        RemoteDMATransfer(dst_ids=[dst(peer - RANK_CORE + PORT_CORE), dst(peer)], dma_engine_mask=0x000F,
-                          remote_sem=s.rin, srcs=[T.xs[:]], dsts=[T.hb[:], T.rp[:]]),
-        RemoteDMATransfer(dst_ids=[dst(c) for c in cols], dma_engine_mask=0x00F0, remote_sem=s.cin,
-                          srcs=[T.xs[:]], dsts=[T.c1[:], T.c2[:], T.c3[:]]),
-    ], local_sem=s.sent)
+    sends = []
+    for q in range(4):
+        ids, outs = [dst(chip ^ 2, PORT_CORE)], [T.hb[q]]
+        if q != row:
+            ids.append(dst(4 * q + col, COL_CORE))
+            outs.append(T.cq[row])
+        ids.append(dst(chip ^ 2, RANK_CORE))
+        outs.append(T.rp[q])
+        sends.append(RemoteDMATransfer(dst_ids=ids, dma_engine_mask=3 << (2 * q), remote_sem=s.rin,
+                                       srcs=[T.xs[q]], dsts=outs))
+        ids, outs = [dst(chip, PORT_CORE)], [T.ha[q]]
+        if q == row:
+            ids.append(dst(chip, COL_CORE))
+            outs.append(T.cq[row])
+        sends.append(RemoteDMATransfer(dst_ids=ids, dma_engine_mask=3 << (8 + 2 * q), remote_sem=s.rin,
+                                       srcs=[T.xs[q]], dsts=outs))
+    g.remote_dma_fused(sends, local_sem=s.sent)
 
-    g.wait_ge(s.rin, 4)
+    g.wait_ge(s.rin, 8)
     g.wait_ge(s.k1, 16)
     g.dma_start(out=T.y1[:], in_=T.rp[:], accum_op=add, max_dma_last_dim=8192).then_inc(s.k1, 16)
-    g.wait_ge(s.cin, 12)
-    g.wait_ge(s.k2, 16)
-    g.dma_start(out=T.y2[:], in_=T.c1[:], accum_op=add, max_dma_last_dim=8192).then_inc(s.k2, 16)
-    g.dma_start(out=T.c2[:], in_=T.c3[:], accum_op=add, max_dma_last_dim=8192).then_inc(s.k3, 16)
-    g.wait_ge(s.k2, 32)
-    g.wait_ge(s.k3, 16)
-    g.dma_start(out=T.y2[:], in_=T.c2[:], accum_op=add, max_dma_last_dim=8192).then_inc(s.k2, 16)
+    g.wait_ge(s.cin, 32)
+    g.dma_start(out=T.y2[:], in_=T.ys[:]).then_inc(s.k2, 16)
     g.wait_ge(s.pin, 8)
     g.wait_ge(s.k1, 32)
     g.dma_start(out=T.y1[:], in_=T.pm[:], accum_op=add, max_dma_last_dim=8192).then_inc(s.k1, 16)
     g.wait_ge(s.k1, 48)
-    g.wait_ge(s.k2, 48)
+    g.wait_ge(s.k2, 16)
     g.wait_ge(s.sent, 16)

@@ -1,37 +1,42 @@
 from concourse.bass import DstId, RemoteDMATransfer
-from concourse.mybir import AluOpType
 
 BUF = ("dram", [4, 128, 32], "float32")
 SCRATCH = {
     "xs": BUF,
-    "rp": BUF,
-    "pm": BUF,
+    "rs": BUF,
     "ys": BUF,
     "ha": BUF, "hb": BUF,
+    "pm": BUF,
     "cq": BUF,
 }
-SEMAPHORES = ["ld", "k1", "k2", "rin", "cin", "pin", "sent"]
+SEMAPHORES = ["ld", "k1", "k2", "rin", "cin", "pin", "yin", "sent"]
 
-RANK_CORE, PORT_CORE, COL_CORE = 1, 2, 4
+RANK_CORE, COL_CORE = 1, 4
+PORT_CORES = (2, 6, 3, 7)
 
 
 def rank_program(g, core, T, topo):
     chip, k = core // 8, core % 8
     s = T.sem
-    add = AluOpType.add
     row, col = chip // 4, chip % 4
 
     def dst(ch, kk):
         rid, pid, se = topo.addr(ch * 8 + kk)
         return DstId(rid=rid, pnc=pid)
 
-    if k == PORT_CORE:
-        g.wait_ge(s.rin, 16)
+    if k in PORT_CORES:
+        q = PORT_CORES.index(k)
+        g.wait_ge(s.rin, 4)
         g.remote_dma_fused([
-            RemoteDMATransfer(dst_ids=[dst(chip ^ 1, RANK_CORE)], dma_engine_mask=3 << (2 * q), remote_sem=s.pin,
-                              srcs=[T.ha[q], T.hb[q]], dsts=[T.pm[q]], alu_op=1)
-            for q in range(4)], local_sem=s.sent)
-        g.wait_ge(s.sent, 8)
+            RemoteDMATransfer(dst_ids=[dst(chip ^ 1, k)], dma_engine_mask=0x00FF, remote_sem=s.pin,
+                              srcs=[T.ha[q], T.hb[q]], dsts=[T.pm[q]], alu_op=1),
+        ], local_sem=s.sent)
+        g.wait_ge(s.pin, 8)
+        g.remote_dma_fused([
+            RemoteDMATransfer(dst_ids=[dst(chip, RANK_CORE)], dma_engine_mask=0xFFFF, remote_sem=s.yin,
+                              srcs=[T.ha[q], T.hb[q], T.pm[q]], dsts=[T.rs[q]], alu_op=1),
+        ], local_sem=s.sent)
+        g.wait_ge(s.sent, 24)
         return
     if k == COL_CORE:
         g.wait_ge(s.rin, 8)
@@ -46,19 +51,16 @@ def rank_program(g, core, T, topo):
         return
 
     g.dma_start(out=T.xs[:], in_=T.x[:]).then_inc(s.ld, 16)
-    g.dma_start(out=T.y1[:], in_=T.x[:]).then_inc(s.k1, 16)
     g.wait_ge(s.ld, 16)
     sends = []
     for q in range(4):
-        ids, outs = [dst(chip ^ 2, PORT_CORE)], [T.hb[q]]
+        ids, outs = [dst(chip ^ 2, PORT_CORES[q])], [T.hb[q]]
         if q != row:
             ids.append(dst(4 * q + col, COL_CORE))
             outs.append(T.cq[row])
-        ids.append(dst(chip ^ 2, RANK_CORE))
-        outs.append(T.rp[q])
         sends.append(RemoteDMATransfer(dst_ids=ids, dma_engine_mask=3 << (2 * q), remote_sem=s.rin,
                                        srcs=[T.xs[q]], dsts=outs))
-        ids, outs = [dst(chip, PORT_CORE)], [T.ha[q]]
+        ids, outs = [dst(chip, PORT_CORES[q])], [T.ha[q]]
         if q == row:
             ids.append(dst(chip, COL_CORE))
             outs.append(T.cq[row])
@@ -66,14 +68,10 @@ def rank_program(g, core, T, topo):
                                        srcs=[T.xs[q]], dsts=outs))
     g.remote_dma_fused(sends, local_sem=s.sent)
 
-    g.wait_ge(s.rin, 8)
-    g.wait_ge(s.k1, 16)
-    g.dma_start(out=T.y1[:], in_=T.rp[:], accum_op=add, max_dma_last_dim=8192).then_inc(s.k1, 16)
     g.wait_ge(s.cin, 32)
     g.dma_start(out=T.y2[:], in_=T.ys[:]).then_inc(s.k2, 16)
-    g.wait_ge(s.pin, 8)
-    g.wait_ge(s.k1, 32)
-    g.dma_start(out=T.y1[:], in_=T.pm[:], accum_op=add, max_dma_last_dim=8192).then_inc(s.k1, 16)
-    g.wait_ge(s.k1, 48)
+    g.wait_ge(s.yin, 64)
+    g.dma_start(out=T.y1[:], in_=T.rs[:]).then_inc(s.k1, 16)
     g.wait_ge(s.k2, 16)
+    g.wait_ge(s.k1, 16)
     g.wait_ge(s.sent, 16)

@@ -12,20 +12,21 @@ SCRATCH = {
 SEMAPHORES = ["ld", "k1", "k2", "rin", "cin", "pin", "yin", "sent"]
 
 RANK_CORE, COL_CORE = 1, 4
-PORT_CORES = (2, 6, 3, 7)
+PORT_CORES = (2, 6)
 
 
 def rank_program(g, core, T, topo):
     chip, k = core // 8, core % 8
     s = T.sem
     row, col = chip // 4, chip % 4
+    pair = (chip >> 1) & 1
 
     def dst(ch, kk):
         rid, pid, se = topo.addr(ch * 8 + kk)
         return DstId(rid=rid, pnc=pid)
 
     if k in PORT_CORES:
-        q = PORT_CORES.index(k)
+        q = 2 * pair + PORT_CORES.index(k)
         g.wait_ge(s.rin, 4)
         g.remote_dma_fused([
             RemoteDMATransfer(dst_ids=[dst(chip ^ 1, k)], dma_engine_mask=0x00FF, remote_sem=s.pin,
@@ -33,9 +34,9 @@ def rank_program(g, core, T, topo):
         ], local_sem=s.sent)
         g.wait_ge(s.pin, 8)
         g.remote_dma_fused([
-            RemoteDMATransfer(dst_ids=[dst(chip, RANK_CORE)], dma_engine_mask=0xFFFF, remote_sem=s.yin,
-                              srcs=[T.ha[q], T.hb[q], T.pm[q]], dsts=[T.rs[q]], alu_op=1),
-        ], local_sem=s.sent)
+            RemoteDMATransfer(dst_ids=[dst(ch, RANK_CORE)], dma_engine_mask=m, remote_sem=s.yin,
+                              srcs=[T.ha[q], T.hb[q], T.pm[q]], dsts=[T.rs[q]], alu_op=1)
+            for ch, m in ((chip ^ 2, 0x00FF), (chip, 0xFF00))], local_sem=s.sent)
         g.wait_ge(s.sent, 24)
         return
     if k == COL_CORE:
@@ -54,24 +55,26 @@ def rank_program(g, core, T, topo):
     g.wait_ge(s.ld, 16)
     sends = []
     for q in range(4):
-        ids, outs = [dst(chip ^ 2, PORT_CORES[q])], [T.hb[q]]
-        if q != row:
-            ids.append(dst(4 * q + col, COL_CORE))
-            outs.append(T.cq[row])
-        sends.append(RemoteDMATransfer(dst_ids=ids, dma_engine_mask=3 << (2 * q), remote_sem=s.rin,
-                                       srcs=[T.xs[q]], dsts=outs))
-        ids, outs = [dst(chip, PORT_CORES[q])], [T.ha[q]]
+        far, near = [], []
+        owner = PORT_CORES[q % 2]
+        if q // 2 == pair:
+            near.append((dst(chip, owner), T.ha[q]))
+        else:
+            far.append((dst(chip ^ 2, owner), T.hb[q]))
         if q == row:
-            ids.append(dst(chip, COL_CORE))
-            outs.append(T.cq[row])
-        sends.append(RemoteDMATransfer(dst_ids=ids, dma_engine_mask=3 << (8 + 2 * q), remote_sem=s.rin,
-                                       srcs=[T.xs[q]], dsts=outs))
+            near.append((dst(chip, COL_CORE), T.cq[row]))
+        else:
+            far.append((dst(4 * q + col, COL_CORE), T.cq[row]))
+        for lst, shift in ((far, 2 * q), (near, 8 + 2 * q)):
+            if lst:
+                sends.append(RemoteDMATransfer(dst_ids=[d for d, b in lst], dma_engine_mask=3 << shift,
+                                               remote_sem=s.rin, srcs=[T.xs[q]], dsts=[b for d, b in lst]))
     g.remote_dma_fused(sends, local_sem=s.sent)
 
     g.wait_ge(s.cin, 32)
     g.dma_start(out=T.y2[:], in_=T.ys[:]).then_inc(s.k2, 16)
-    g.wait_ge(s.yin, 64)
+    g.wait_ge(s.yin, 32)
     g.dma_start(out=T.y1[:], in_=T.rs[:]).then_inc(s.k1, 16)
     g.wait_ge(s.k2, 16)
     g.wait_ge(s.k1, 16)
-    g.wait_ge(s.sent, 16)
+    g.wait_ge(s.sent, 2 * len(sends))

from concourse.bass import DstId, RemoteDMATransfer

BUF = ("dram", [4, 128, 32], "float32")
SCRATCH = {
    "xs": BUF,
    "rs": BUF,
    "ys": BUF,
    "ha": BUF, "hb": BUF,
    "pm": BUF,
    "cq": BUF,
}
SEMAPHORES = ["ld", "k1", "k2", "rin", "cin", "pin", "yin", "sent"]

RANK_CORE, COL_CORE = 1, 4
PORT_CORES = (2, 6)


def rank_program(g, core, T, topo):
    chip, k = core // 8, core % 8
    s = T.sem
    row, col = chip // 4, chip % 4
    pair = (chip >> 1) & 1

    def dst(ch, kk):
        rid, pid, se = topo.addr(ch * 8 + kk)
        return DstId(rid=rid, pnc=pid)

    if k in PORT_CORES:
        q = 2 * pair + PORT_CORES.index(k)
        g.wait_ge(s.rin, 4)
        g.remote_dma_fused([
            RemoteDMATransfer(dst_ids=[dst(chip ^ 1, k)], dma_engine_mask=0x00FF, remote_sem=s.pin,
                              srcs=[T.ha[q], T.hb[q]], dsts=[T.pm[q]], alu_op=1),
        ], local_sem=s.sent)
        g.wait_ge(s.pin, 8)
        g.remote_dma_fused([
            RemoteDMATransfer(dst_ids=[dst(ch, RANK_CORE)], dma_engine_mask=m, remote_sem=s.yin,
                              srcs=[T.ha[q], T.hb[q], T.pm[q]], dsts=[T.rs[q]], alu_op=1)
            for ch, m in ((chip ^ 2, 0x00FF), (chip, 0xFF00))], local_sem=s.sent)
        g.wait_ge(s.sent, 24)
        return
    if k == COL_CORE:
        g.wait_ge(s.rin, 8)
        others = [i for i in range(4) if i != row]
        g.remote_dma_fused([
            RemoteDMATransfer(dst_ids=[dst(4 * i + col, RANK_CORE) for i in others + [row]], dma_engine_mask=0x00FF,
                              remote_sem=s.cin, srcs=[T.cq[i] for i in range(4)], dsts=[T.ys[row]] * 4, alu_op=1),
        ], local_sem=s.sent)
        g.wait_ge(s.sent, 8)
        return
    if k != RANK_CORE:
        return

    g.dma_start(out=T.xs[:], in_=T.x[:]).then_inc(s.ld, 16)
    g.wait_ge(s.ld, 16)
    sends = []
    for q in range(4):
        far, near = [], []
        owner = PORT_CORES[q % 2]
        if q // 2 == pair:
            near.append((dst(chip, owner), T.ha[q]))
        else:
            far.append((dst(chip ^ 2, owner), T.hb[q]))
        if q == row:
            near.append((dst(chip, COL_CORE), T.cq[row]))
        else:
            far.append((dst(4 * q + col, COL_CORE), T.cq[row]))
        for lst, shift in ((far, 2 * q), (near, 8 + 2 * q)):
            if lst:
                sends.append(RemoteDMATransfer(dst_ids=[d for d, b in lst], dma_engine_mask=3 << shift,
                                               remote_sem=s.rin, srcs=[T.xs[q]], dsts=[b for d, b in lst]))
    g.remote_dma_fused(sends, local_sem=s.sent)

    g.wait_ge(s.cin, 32)
    g.dma_start(out=T.y2[:], in_=T.ys[:]).then_inc(s.k2, 16)
    g.wait_ge(s.yin, 32)
    g.dma_start(out=T.y1[:], in_=T.rs[:]).then_inc(s.k1, 16)
    g.wait_ge(s.k2, 16)
    g.wait_ge(s.k1, 16)
    g.wait_ge(s.sent, 2 * len(sends))
